import numpy as np, ml_dtypes
CORES = [45,53,77,117,47,55,79,119]
N = 8
DEG, TK, TIMES = 3, 256, 2
MASK = [[0,3,6],[0,1,5],[0,2,3],[1,3,6],[4,5,7],[1,5,6],[1,3,6],[2,4,7]]
def setup_inputs(rng):
    return {"x": rng.standard_normal((N, 128, TK), dtype=np.float32).astype(ml_dtypes.bfloat16), "w": (rng.standard_normal((N, 128, DEG * 128), dtype=np.float32) / np.float32(np.sqrt(128 * DEG / 2))).astype(ml_dtypes.bfloat16)}
def setup_inputs_big(rng):
    d = setup_inputs(rng)
    for k in ("x",): d[k] = (d[k].astype(np.float32) * 1048576.0).astype(d[k].dtype)
    return d
def setup_inputs_small(rng):
    d = setup_inputs(rng)
    for k in ("x",): d[k] = (d[k].astype(np.float32) * (1 / 1048576.0)).astype(d[k].dtype)
    return d
def setup_inputs_apart(rng):
    d = setup_inputs(rng)
    f = (10.0 ** rng.permutation(np.linspace(-1.5, 1.5, N))).astype(np.float32).reshape(N, 1, 1)
    for k in ("x",): d[k] = (d[k].astype(np.float32) * f).astype(d[k].dtype)
    return d
def reference(x, w):
    X, W = x.astype(np.float64), w.astype(np.float64)
    h = list(X)
    for _ in range(TIMES):
        h = [np.maximum(sum(W[r][:, 128 * i:128 * i + 128].T @ h[j] for i, j in enumerate(MASK[r])), 0.0) for r in range(N)]
    return {"y": np.stack(h).astype(ml_dtypes.bfloat16)}

@@ -1,0 +1,238 @@
+from concourse.bass import DstId, RemoteDMATransfer
+from concourse.mybir import AluOpType
+
+N, P, TK, DEG = 8, 128, 256, 3
+XW = TK + DEG * P
+
+CFG = {
+    "site": {j: [(j, -2)] for j in range(N)},
+    "relay": {k: [(k, -2)] for k in range(N)},
+    "hslot": [0, 1, 2, 3, 6, 5, 4, 7],
+    "pack_off": True, "pack_relay": False, "pack_on": False, "hpack": True, "on_eng": 16,
+}
+
+SCRATCH = {"hh": ("sbuf", [P, N * TK], "bfloat16"), "yo": ("sbuf", [P, TK], "bfloat16"),
+           "zero": ("sbuf", [P, TK], "float32")}
+for _k in range(N):
+    SCRATCH["xw%d" % _k] = ("sbuf", [P, XW], "bfloat16")
+for _k in range(5):
+    SCRATCH["ps%d" % _k] = ("psum", [P, 512], "float32")
+SEMAPHORES = ["sent", "zs", "sy", "st"] + ["mm%d" % i for i in range(5)] + \
+             ["s%s%d" % (a, k) for a in "xwphq" for k in range(N)]
+
+
+def _bits(m):
+    return bin(m).count("1")
+
+
+def _plan(T, topo, cfg):
+    cores, M = list(T.cores), T.tables["MASK"]
+    allc = range(topo.CHIPS * topo.CORES_PER_CHIP)
+
+    def owner(c):
+        return all(topo.may_write(c, d) for d in cores if d != c)
+
+    def slot(a, s):
+        home = cores[a]
+        if s == -1 or (s == -2 and owner(home)):
+            return home
+        if s == -2:
+            return [c for c in cores if topo.chip(c) == topo.chip(home) and owner(c)][0]
+        hs = [c for c in allc if topo.chip(c) == topo.chip(home) and c not in cores and owner(c)]
+        hs.sort(key=lambda c: (topo.die(c) != topo.die(home), c))
+        return hs[s]
+
+    site = {j: [slot(a, s) for a, s in cfg["site"][j]] for j in range(N)}
+    relay = {k: [slot(a, s) for a, s in v] for k, v in cfg["relay"].items()}
+    hpos = {j: cfg["hslot"].index(j) for j in range(N)}
+    est, avail, sends, groups = {}, {}, {}, {}
+
+    def add_send(src, parts, dests):
+        start = max(est[(src, p)] for p in parts)
+        off = [d for d in dests if topo.chip(d) != topo.chip(src)]
+        on = [d for d in dests if topo.chip(d) == topo.chip(src)]
+        kind = parts[0][0]
+        if len(parts) > 1:
+            kind = "p" if kind == "x" else "q"
+        sem = "s%s%d" % (kind, parts[0][1])
+        trs = []
+        m_off = 0
+        if off:
+            m_off = topo.mask(src, off[0])
+            trs.append((off, m_off))
+        if on:
+            m_on = topo.mask(src, on[0]) & ~m_off
+            if _bits(m_on) > cfg["on_eng"]:
+                keep, mm = 0, 0
+                for b in range(16):
+                    if (m_on >> b) & 1 and keep < cfg["on_eng"]:
+                        mm |= 1 << b
+                        keep += 1
+                m_on = mm
+            trs.append((on, m_on))
+        width = sum(TK if p[0] != "w" else DEG * P for p in parts)
+        for ds, m in trs:
+            for i, d in enumerate(ds):
+                assert topo.may_write(src, d), (src, d)
+                for p in parts:
+                    assert (d, p) not in est, (d, p)
+                    est[(d, p)] = start + 1.0 + width / 1024.0 * (i + 1) * (1.0 if ds is off else 0.5)
+                    avail[(d, p)] = [(sem, _bits(m))]
+        sends.setdefault(src, []).append((start, len(sends.get(src, [])), parts, trs, sem))
+
+    need = {}
+    for j in range(N):
+        for s in site[j]:
+            need.setdefault(s, set()).update([("x", k) for k in M[j]] + [("w", j)])
+    for k in range(N):
+        home = cores[k]
+        est[(home, ("x", k))], est[(home, ("w", k))] = 0.0, 0.2
+        avail[(home, ("x", k))], avail[(home, ("w", k))] = [("sx%d" % k, 16)], [("sw%d" % k, 16)]
+
+    def fan(src, k, want):
+        px, pw, pp = [], [], []
+        for d in sorted(want, key=lambda d: (topo.chip(d) == topo.chip(src), d)):
+            ks = want[d]
+            pol = cfg["pack_on"] if topo.chip(d) == topo.chip(src) else cfg["pack_off"]
+            if src != cores[k]:
+                pol = cfg["pack_relay"]
+            if len(ks) == 2 and pol:
+                pp.append(d)
+            else:
+                if "x" in ks:
+                    px.append(d)
+                if "w" in ks:
+                    pw.append(d)
+        if px:
+            add_send(src, [("x", k)], px)
+        if pp:
+            add_send(src, [("x", k), ("w", k)], pp)
+        if pw:
+            add_send(src, [("w", k)], pw)
+
+    fwd = {}
+    for k in range(N):
+        home = cores[k]
+        direct = {}
+        far = sorted(set(topo.chip(c) for c in need if c != home and not topo.may_write(home, c)))
+        for c in sorted(need):
+            if c == home:
+                continue
+            ks = set(a for a in "xw" if (a, k) in need[c])
+            if not ks:
+                continue
+            if topo.may_write(home, c):
+                direct.setdefault(c, set()).update(ks)
+            else:
+                r = relay[k][far.index(topo.chip(c)) % len(relay[k])]
+                direct.setdefault(r, set()).update(ks)
+                fwd.setdefault((r, k), {})[c] = ks
+        fan(home, k, direct)
+    for (r, k), want in sorted(fwd.items()):
+        fan(r, k, want)
+
+    for j in range(N):
+        for s in site[j]:
+            mms = [(max(est[(s, ("x", k))], est[(s, ("w", j))]), i, ("w", j), ("x", k)) for i, k in enumerate(M[j])]
+            t = max(m[0] for m in mms) + 0.2
+            est[(s, ("h", j))] = t
+            avail[(s, ("h", j))] = [("sh%d" % j, 1)]
+            groups.setdefault(s, []).append((t, ("h", j), sorted(mms)))
+    hs = {}
+    for r in range(N):
+        for j in M[r]:
+            if cores[r] in site[j]:
+                continue
+            ok = [s for s in site[j] if topo.may_write(s, cores[r])]
+            ok.sort(key=lambda s: (topo.chip(s) != topo.chip(cores[r]),
+                                   not topo.same_plane(topo.chip(s), topo.chip(cores[r]))))
+            hs.setdefault(ok[0], {}).setdefault(cores[r], []).append(j)
+    for s in sorted(hs):
+        bund = {}
+        for d, js in hs[s].items():
+            js = sorted(js, key=lambda j: hpos[j])
+            runs = [[js[0]]]
+            for j in js[1:]:
+                if cfg["hpack"] and hpos[j] == hpos[runs[-1][-1]] + 1:
+                    runs[-1].append(j)
+                else:
+                    runs.append([j])
+            for run in runs:
+                bund.setdefault(tuple(run), []).append(d)
+        for run in sorted(bund, key=lambda run: max(est[(s, ("h", j))] for j in run)):
+            add_send(s, [("h", j) for j in run], sorted(bund[run], key=lambda d: (topo.chip(d) == topo.chip(s), d)))
+    for r in range(N):
+        c = cores[r]
+        mms = [(max(est[(c, ("h", j))], est[(c, ("w", r))]), i, ("w", r), ("h", j)) for i, j in enumerate(M[r])]
+        groups.setdefault(c, []).append((max(m[0] for m in mms) + 0.2, ("y", r), sorted(mms)))
+    return sends, groups, avail, hpos
+
+
+def rank_program(g, core, T, topo):
+    sends, groups, avail, hpos = _plan(T, topo, CFG)
+    rank = T.rank_of(core)
+
+    def ap(item):
+        a, k = item
+        if a == "x":
+            return T["xw%d" % k], 0, TK
+        if a == "w":
+            return T["xw%d" % k], TK, XW
+        return T.hh, hpos[k] * TK, hpos[k] * TK + TK
+
+    def waiter(q):
+        seen = set()
+
+        def w(items):
+            for it in items:
+                for sem, n in avail[(core, it)]:
+                    if sem not in seen:
+                        seen.add(sem)
+                        q.wait_ge(T.sem[sem], n)
+        return w
+
+    if rank is not None:
+        g.sync.dma_start(T["xw%d" % rank][:, 0:TK], T.x[:, :]).then_inc(T.sem["sx%d" % rank], 16)
+        g.scalar.dma_start(T["xw%d" % rank][:, TK:XW], T.w[:, :]).then_inc(T.sem["sw%d" % rank], 16)
+
+    gw, total = waiter(g), 0
+    for _, _, parts, trs, sem in sorted(sends.get(core, [])):
+        gw(parts)
+        buf, lo, _ = ap(parts[0])
+        hi = ap(parts[-1])[2]
+        lst = []
+        for ds, m in trs:
+            ids = [DstId(rid=topo.addr(d)[0], pnc=topo.addr(d)[1]) for d in ds]
+            lst.append(RemoteDMATransfer(dst_ids=ids, dma_engine_mask=m, remote_sem=T.sem[sem],
+                                         srcs=[buf[:, lo:hi]], dsts=[buf[:, lo:hi] for _ in ds]))
+            total += _bits(m)
+        g.remote_dma_fused(lst, local_sem=T.sem.sent)
+    if total:
+        g.wait_ge(T.sem.sent, total)
+
+    gs = sorted(groups.get(core, []))
+    if gs:
+        g.vector.memset(T.zero[:, :], 0.0).then_inc(T.sem.zs, 1)
+        g.vector.wait_ge(T.sem.zs, 1)
+        tw = waiter(g.tensor)
+        todo = sorted((m[0], b, n, m) for b, (_, _, mms) in enumerate(gs) for n, m in enumerate(mms))
+        for _, b, n, (_, i, wi, hi_) in todo:
+            tw([wi, hi_])
+            wb, wlo, _ = ap(wi)
+            hb, hlo, hhi = ap(hi_)
+            ins = g.tensor.matmul(T["ps%d" % b][:, 0:TK], wb[:, wlo + P * i:wlo + P * i + P], hb[:, hlo:hhi],
+                                  n == 0, n == DEG - 1)
+            if n == DEG - 1:
+                ins.then_inc(T.sem["mm%d" % b], 1)
+        for b, (_, out, _) in enumerate(gs):
+            g.vector.wait_ge(T.sem["mm%d" % b], 1)
+            if out[0] == "h":
+                ob, lo, hi = ap(out)
+                g.vector.tensor_tensor(ob[:, lo:hi], T["ps%d" % b][:, 0:TK], T.zero[:, :],
+                                       AluOpType.max).then_inc(T.sem["sh%d" % out[1]], 1)
+            else:
+                g.vector.tensor_tensor(T.yo[:, :], T["ps%d" % b][:, 0:TK], T.zero[:, :],
+                                       AluOpType.max).then_inc(T.sem.sy, 1)
+                g.sync.wait_ge(T.sem.sy, 1)
+                g.sync.dma_start(T.y[:, :], T.yo[:, :]).then_inc(T.sem.st, 16)
+                g.sync.wait_ge(T.sem.st, 16)

@@ -7,9 +7,12 @@ XW = TK + DEG * P
 CFG = {
     "site": {j: [(j, -2)] for j in range(N)},
     "relay": {k: [(k, -2)] for k in range(N)},
+    "via": {(6, 0): (2, -1)},
     "hslot": [0, 1, 2, 3, 6, 5, 4, 7],
-    "pack_off": True, "pack_relay": False, "pack_on": False, "hpack": True, "on_eng": 16,
+    "pack_off": False, "pack_relay": False, "pack_on": False, "hpack": False, "on_eng": 16,
+    "keep_off": True, "split": True, "w_late": 1.3,
 }
+CFG["site"][6] = [(6, -2), (7, -2)]
 
 SCRATCH = {"hh": ("sbuf", [P, N * TK], "bfloat16"), "yo": ("sbuf", [P, TK], "bfloat16"),
            "zero": ("sbuf", [P, TK], "float32")}
@@ -49,6 +52,8 @@ def _plan(T, topo, cfg):
 
     def add_send(src, parts, dests):
         start = max(est[(src, p)] for p in parts)
+        if parts[0][0] == "w" and any(topo.chip(d) != topo.chip(src) for d in dests):
+            start = max(start, cfg["w_late"])
         off = [d for d in dests if topo.chip(d) != topo.chip(src)]
         on = [d for d in dests if topo.chip(d) == topo.chip(src)]
         kind = parts[0][0]
@@ -62,6 +67,8 @@ def _plan(T, topo, cfg):
             trs.append((off, m_off))
         if on:
             m_on = topo.mask(src, on[0]) & ~m_off
+            if cfg["keep_off"] and owner(src):
+                m_on = m_on & ~min(topo.mask(src, d) for d in cores if topo.chip(d) != topo.chip(src))
             if _bits(m_on) > cfg["on_eng"]:
                 keep, mm = 0, 0
                 for b in range(16):
@@ -78,7 +85,9 @@ def _plan(T, topo, cfg):
                     assert (d, p) not in est, (d, p)
                     est[(d, p)] = start + 1.0 + width / 1024.0 * (i + 1) * (1.0 if ds is off else 0.5)
                     avail[(d, p)] = [(sem, _bits(m))]
-        sends.setdefault(src, []).append((start, len(sends.get(src, [])), parts, trs, sem))
+        calls = [[t] for t in trs] if cfg["split"] and owner(src) else [trs]
+        for c in calls:
+            sends.setdefault(src, []).append((start, len(sends.get(src, [])), parts, c, sem))
 
     need = {}
     for j in range(N):
@@ -91,7 +100,7 @@ def _plan(T, topo, cfg):
 
     def fan(src, k, want):
         px, pw, pp = [], [], []
-        for d in sorted(want, key=lambda d: (topo.chip(d) == topo.chip(src), d)):
+        for d in sorted(want, key=lambda d: (topo.chip(d) == topo.chip(src), -urgency(d, k), d)):
             ks = want[d]
             pol = cfg["pack_on"] if topo.chip(d) == topo.chip(src) else cfg["pack_off"]
             if src != cores[k]:
@@ -110,7 +119,12 @@ def _plan(T, topo, cfg):
         if pw:
             add_send(src, [("w", k)], pw)
 
-    fwd = {}
+    def urgency(d, k):
+        u = sum(1 for j in range(N) if d in site[j] and k in M[j]
+                for r in range(N) if j in M[r] and topo.chip(cores[r]) != topo.chip(d))
+        return u + sum(1 + urgency(c, k) for (r, kk), v in fwd.items() if r == d and kk == k for c in v)
+
+    fwd, first = {}, []
     for k in range(N):
         home = cores[k]
         direct = {}
@@ -121,12 +135,19 @@ def _plan(T, topo, cfg):
             ks = set(a for a in "xw" if (a, k) in need[c])
             if not ks:
                 continue
-            if topo.may_write(home, c):
+            via = [slot(b, s) for (kk, a), (b, s) in cfg["via"].items()
+                   if kk == k and topo.chip(cores[a]) == topo.chip(c)]
+            if via:
+                direct.setdefault(via[0], set()).update(ks)
+                fwd.setdefault((via[0], k), {})[c] = ks
+            elif topo.may_write(home, c):
                 direct.setdefault(c, set()).update(ks)
             else:
                 r = relay[k][far.index(topo.chip(c)) % len(relay[k])]
                 direct.setdefault(r, set()).update(ks)
                 fwd.setdefault((r, k), {})[c] = ks
+        first.append((home, k, direct))
+    for home, k, direct in first:
         fan(home, k, direct)
     for (r, k), want in sorted(fwd.items()):
         fan(r, k, want)
@@ -144,8 +165,7 @@ def _plan(T, topo, cfg):
             if cores[r] in site[j]:
                 continue
             ok = [s for s in site[j] if topo.may_write(s, cores[r])]
-            ok.sort(key=lambda s: (topo.chip(s) != topo.chip(cores[r]),
-                                   not topo.same_plane(topo.chip(s), topo.chip(cores[r]))))
+            ok.sort(key=lambda s: (topo.chip(s) != topo.chip(cores[r]), site[j].index(s)))
             hs.setdefault(ok[0], {}).setdefault(cores[r], []).append(j)
     for s in sorted(hs):
         bund = {}
@@ -159,7 +179,8 @@ def _plan(T, topo, cfg):
                     runs.append([j])
             for run in runs:
                 bund.setdefault(tuple(run), []).append(d)
-        for run in sorted(bund, key=lambda run: max(est[(s, ("h", j))] for j in run)):
+        for run in sorted(bund, key=lambda run: (max(est[(s, ("h", j))] for j in run),
+                                                 sum(1 for d in bund[run] if topo.chip(d) != topo.chip(s)))):
             add_send(s, [("h", j) for j in run], sorted(bund[run], key=lambda d: (topo.chip(d) == topo.chip(s), d)))
     for r in range(N):
         c = cores[r]

from concourse.bass import DstId, RemoteDMATransfer
from concourse.mybir import AluOpType

N, P, TK, DEG = 8, 128, 256, 3
XW = TK + DEG * P

CFG = {
    "site": {j: [(j, -2)] for j in range(N)},
    "relay": {k: [(k, -2)] for k in range(N)},
    "via": {(6, 0): (2, -1)},
    "hslot": [0, 1, 2, 3, 6, 5, 4, 7],
    "pack_off": False, "pack_relay": False, "pack_on": False, "hpack": False, "on_eng": 16,
    "keep_off": True, "split": True, "w_late": 1.3,
}
CFG["site"][6] = [(6, -2), (7, -2)]

SCRATCH = {"hh": ("sbuf", [P, N * TK], "bfloat16"), "yo": ("sbuf", [P, TK], "bfloat16"),
           "zero": ("sbuf", [P, TK], "float32")}
for _k in range(N):
    SCRATCH["xw%d" % _k] = ("sbuf", [P, XW], "bfloat16")
for _k in range(5):
    SCRATCH["ps%d" % _k] = ("psum", [P, 512], "float32")
SEMAPHORES = ["sent", "zs", "sy", "st"] + ["mm%d" % i for i in range(5)] + \
             ["s%s%d" % (a, k) for a in "xwphq" for k in range(N)]


def _bits(m):
    return bin(m).count("1")


def _plan(T, topo, cfg):
    cores, M = list(T.cores), T.tables["MASK"]
    allc = range(topo.CHIPS * topo.CORES_PER_CHIP)

    def owner(c):
        return all(topo.may_write(c, d) for d in cores if d != c)

    def slot(a, s):
        home = cores[a]
        if s == -1 or (s == -2 and owner(home)):
            return home
        if s == -2:
            return [c for c in cores if topo.chip(c) == topo.chip(home) and owner(c)][0]
        hs = [c for c in allc if topo.chip(c) == topo.chip(home) and c not in cores and owner(c)]
        hs.sort(key=lambda c: (topo.die(c) != topo.die(home), c))
        return hs[s]

    site = {j: [slot(a, s) for a, s in cfg["site"][j]] for j in range(N)}
    relay = {k: [slot(a, s) for a, s in v] for k, v in cfg["relay"].items()}
    hpos = {j: cfg["hslot"].index(j) for j in range(N)}
    est, avail, sends, groups = {}, {}, {}, {}

    def add_send(src, parts, dests):
        start = max(est[(src, p)] for p in parts)
        if parts[0][0] == "w" and any(topo.chip(d) != topo.chip(src) for d in dests):
            start = max(start, cfg["w_late"])
        off = [d for d in dests if topo.chip(d) != topo.chip(src)]
        on = [d for d in dests if topo.chip(d) == topo.chip(src)]
        kind = parts[0][0]
        if len(parts) > 1:
            kind = "p" if kind == "x" else "q"
        sem = "s%s%d" % (kind, parts[0][1])
        trs = []
        m_off = 0
        if off:
            m_off = topo.mask(src, off[0])
            trs.append((off, m_off))
        if on:
            m_on = topo.mask(src, on[0]) & ~m_off
            if cfg["keep_off"] and owner(src):
                m_on = m_on & ~min(topo.mask(src, d) for d in cores if topo.chip(d) != topo.chip(src))
            if _bits(m_on) > cfg["on_eng"]:
                keep, mm = 0, 0
                for b in range(16):
                    if (m_on >> b) & 1 and keep < cfg["on_eng"]:
                        mm |= 1 << b
                        keep += 1
                m_on = mm
            trs.append((on, m_on))
        width = sum(TK if p[0] != "w" else DEG * P for p in parts)
        for ds, m in trs:
            for i, d in enumerate(ds):
                assert topo.may_write(src, d), (src, d)
                for p in parts:
                    assert (d, p) not in est, (d, p)
                    est[(d, p)] = start + 1.0 + width / 1024.0 * (i + 1) * (1.0 if ds is off else 0.5)
                    avail[(d, p)] = [(sem, _bits(m))]
        calls = [[t] for t in trs] if cfg["split"] and owner(src) else [trs]
        for c in calls:
            sends.setdefault(src, []).append((start, len(sends.get(src, [])), parts, c, sem))

    need = {}
    for j in range(N):
        for s in site[j]:
            need.setdefault(s, set()).update([("x", k) for k in M[j]] + [("w", j)])
    for k in range(N):
        home = cores[k]
        est[(home, ("x", k))], est[(home, ("w", k))] = 0.0, 0.2
        avail[(home, ("x", k))], avail[(home, ("w", k))] = [("sx%d" % k, 16)], [("sw%d" % k, 16)]

    def fan(src, k, want):
        px, pw, pp = [], [], []
        for d in sorted(want, key=lambda d: (topo.chip(d) == topo.chip(src), -urgency(d, k), d)):
            ks = want[d]
            pol = cfg["pack_on"] if topo.chip(d) == topo.chip(src) else cfg["pack_off"]
            if src != cores[k]:
                pol = cfg["pack_relay"]
            if len(ks) == 2 and pol:
                pp.append(d)
            else:
                if "x" in ks:
                    px.append(d)
                if "w" in ks:
                    pw.append(d)
        if px:
            add_send(src, [("x", k)], px)
        if pp:
            add_send(src, [("x", k), ("w", k)], pp)
        if pw:
            add_send(src, [("w", k)], pw)

    def urgency(d, k):
        u = sum(1 for j in range(N) if d in site[j] and k in M[j]
                for r in range(N) if j in M[r] and topo.chip(cores[r]) != topo.chip(d))
        return u + sum(1 + urgency(c, k) for (r, kk), v in fwd.items() if r == d and kk == k for c in v)

    fwd, first = {}, []
    for k in range(N):
        home = cores[k]
        direct = {}
        far = sorted(set(topo.chip(c) for c in need if c != home and not topo.may_write(home, c)))
        for c in sorted(need):
            if c == home:
                continue
            ks = set(a for a in "xw" if (a, k) in need[c])
            if not ks:
                continue
            via = [slot(b, s) for (kk, a), (b, s) in cfg["via"].items()
                   if kk == k and topo.chip(cores[a]) == topo.chip(c)]
            if via:
                direct.setdefault(via[0], set()).update(ks)
                fwd.setdefault((via[0], k), {})[c] = ks
            elif topo.may_write(home, c):
                direct.setdefault(c, set()).update(ks)
            else:
                r = relay[k][far.index(topo.chip(c)) % len(relay[k])]
                direct.setdefault(r, set()).update(ks)
                fwd.setdefault((r, k), {})[c] = ks
        first.append((home, k, direct))
    for home, k, direct in first:
        fan(home, k, direct)
    for (r, k), want in sorted(fwd.items()):
        fan(r, k, want)

    for j in range(N):
        for s in site[j]:
            mms = [(max(est[(s, ("x", k))], est[(s, ("w", j))]), i, ("w", j), ("x", k)) for i, k in enumerate(M[j])]
            t = max(m[0] for m in mms) + 0.2
            est[(s, ("h", j))] = t
            avail[(s, ("h", j))] = [("sh%d" % j, 1)]
            groups.setdefault(s, []).append((t, ("h", j), sorted(mms)))
    hs = {}
    for r in range(N):
        for j in M[r]:
            if cores[r] in site[j]:
                continue
            ok = [s for s in site[j] if topo.may_write(s, cores[r])]
            ok.sort(key=lambda s: (topo.chip(s) != topo.chip(cores[r]), site[j].index(s)))
            hs.setdefault(ok[0], {}).setdefault(cores[r], []).append(j)
    for s in sorted(hs):
        bund = {}
        for d, js in hs[s].items():
            js = sorted(js, key=lambda j: hpos[j])
            runs = [[js[0]]]
            for j in js[1:]:
                if cfg["hpack"] and hpos[j] == hpos[runs[-1][-1]] + 1:
                    runs[-1].append(j)
                else:
                    runs.append([j])
            for run in runs:
                bund.setdefault(tuple(run), []).append(d)
        for run in sorted(bund, key=lambda run: (max(est[(s, ("h", j))] for j in run),
                                                 sum(1 for d in bund[run] if topo.chip(d) != topo.chip(s)))):
            add_send(s, [("h", j) for j in run], sorted(bund[run], key=lambda d: (topo.chip(d) == topo.chip(s), d)))
    for r in range(N):
        c = cores[r]
        mms = [(max(est[(c, ("h", j))], est[(c, ("w", r))]), i, ("w", r), ("h", j)) for i, j in enumerate(M[r])]
        groups.setdefault(c, []).append((max(m[0] for m in mms) + 0.2, ("y", r), sorted(mms)))
    return sends, groups, avail, hpos


def rank_program(g, core, T, topo):
    sends, groups, avail, hpos = _plan(T, topo, CFG)
    rank = T.rank_of(core)

    def ap(item):
        a, k = item
        if a == "x":
            return T["xw%d" % k], 0, TK
        if a == "w":
            return T["xw%d" % k], TK, XW
        return T.hh, hpos[k] * TK, hpos[k] * TK + TK

    def waiter(q):
        seen = set()

        def w(items):
            for it in items:
                for sem, n in avail[(core, it)]:
                    if sem not in seen:
                        seen.add(sem)
                        q.wait_ge(T.sem[sem], n)
        return w

    if rank is not None:
        g.sync.dma_start(T["xw%d" % rank][:, 0:TK], T.x[:, :]).then_inc(T.sem["sx%d" % rank], 16)
        g.scalar.dma_start(T["xw%d" % rank][:, TK:XW], T.w[:, :]).then_inc(T.sem["sw%d" % rank], 16)

    gw, total = waiter(g), 0
    for _, _, parts, trs, sem in sorted(sends.get(core, [])):
        gw(parts)
        buf, lo, _ = ap(parts[0])
        hi = ap(parts[-1])[2]
        lst = []
        for ds, m in trs:
            ids = [DstId(rid=topo.addr(d)[0], pnc=topo.addr(d)[1]) for d in ds]
            lst.append(RemoteDMATransfer(dst_ids=ids, dma_engine_mask=m, remote_sem=T.sem[sem],
                                         srcs=[buf[:, lo:hi]], dsts=[buf[:, lo:hi] for _ in ds]))
            total += _bits(m)
        g.remote_dma_fused(lst, local_sem=T.sem.sent)
    if total:
        g.wait_ge(T.sem.sent, total)

    gs = sorted(groups.get(core, []))
    if gs:
        g.vector.memset(T.zero[:, :], 0.0).then_inc(T.sem.zs, 1)
        g.vector.wait_ge(T.sem.zs, 1)
        tw = waiter(g.tensor)
        todo = sorted((m[0], b, n, m) for b, (_, _, mms) in enumerate(gs) for n, m in enumerate(mms))
        for _, b, n, (_, i, wi, hi_) in todo:
            tw([wi, hi_])
            wb, wlo, _ = ap(wi)
            hb, hlo, hhi = ap(hi_)
            ins = g.tensor.matmul(T["ps%d" % b][:, 0:TK], wb[:, wlo + P * i:wlo + P * i + P], hb[:, hlo:hhi],
                                  n == 0, n == DEG - 1)
            if n == DEG - 1:
                ins.then_inc(T.sem["mm%d" % b], 1)
        for b, (_, out, _) in enumerate(gs):
            g.vector.wait_ge(T.sem["mm%d" % b], 1)
            if out[0] == "h":
                ob, lo, hi = ap(out)
                g.vector.tensor_tensor(ob[:, lo:hi], T["ps%d" % b][:, 0:TK], T.zero[:, :],
                                       AluOpType.max).then_inc(T.sem["sh%d" % out[1]], 1)
            else:
                g.vector.tensor_tensor(T.yo[:, :], T["ps%d" % b][:, 0:TK], T.zero[:, :],
                                       AluOpType.max).then_inc(T.sem.sy, 1)
                g.sync.wait_ge(T.sem.sy, 1)
                g.sync.dma_start(T.y[:, :], T.yo[:, :]).then_inc(T.sem.st, 16)
                g.sync.wait_ge(T.sem.st, 16)
